import numpy as np
import ml_dtypes


def mxq(x, axis, fmt="e4m3"):
    dtype, down = {"e4m3": (ml_dtypes.float8_e4m3fn, 7), "e5m2": (ml_dtypes.float8_e5m2, 14)}[fmt]
    v = np.moveaxis(np.asarray(x, np.float32).astype(ml_dtypes.bfloat16).astype(np.float64), axis, -1)
    blocks = v.reshape(v.shape[:-1] + (-1, 32))
    amax = np.abs(blocks).max(-1, keepdims=True)
    byte = np.maximum(np.where(amax > 0, np.frexp(amax)[1] - 1 + 127, 0) - down, 1)
    scale = np.exp2(byte - 127.0)
    codes = (blocks / scale).astype(np.float32).astype(dtype).astype(np.float64)
    return np.moveaxis((codes * scale).reshape(v.shape), -1, axis)


WIDE = False


def mx_kscale(k):
    if not WIDE:
        return np.ones(k)
    levels = np.array([10, -10, 5, -5, 0])
    if k % 512:
        return np.exp2(np.random.permutation(np.resize(levels, k // 32))).repeat(32)
    a = np.empty((k // 512, 16))
    for p in range(k // 512):
        a[p, :8] = np.random.permutation(np.resize(levels, 8))
        for g in range(8):
            far = levels[np.abs(levels - a[p, g]) >= 10]
            a[p, g + 8] = far[np.random.randint(len(far))]
    return np.exp2(a.ravel()).repeat(32)


def f64(x):
    return np.asarray(x).astype(np.float64)


def striped(idx):
    return np.tile(idx.reshape(-1, 16).T, (8, 1)).astype(np.uint16)


def unstriped(offs):
    return offs[:16].T.reshape(-1).astype(np.int64)


def striped8(idx):
    return np.concatenate([x.reshape(-1, 16).T for x in idx]).astype(np.uint16)


def runs(offs, k):
    lists = np.stack([offs[16 * r : 16 * r + 16].T.reshape(-1) for r in range(8)]).astype(np.int64)
    return lists[np.arange(k) % 512 // 64]


def pack_weight(w):
    k, n = w.shape
    w = f64(np.asarray(w, np.float32).astype(ml_dtypes.bfloat16)).reshape(k // 32, 32, n)
    amax = np.abs(w).max(1)
    byte = np.clip(np.where(amax > 0, np.frexp(amax)[1] - 1 + 127 - 7, 1), 1, 254)
    scaled = (w * np.exp2(127.0 - byte)[:, None, :]).reshape(k, n).astype(np.float32)
    words = np.ascontiguousarray(scaled.reshape(k // 512, 128, 4, n).transpose(0, 1, 3, 2)).astype(ml_dtypes.float8_e4m3fn).view(np.uint8)
    return words, np.ascontiguousarray(byte.astype(np.uint8).reshape(k // 512, 16, n))


def unpack_weight(words, scales):
    g, p, n, _ = words.shape
    vals = np.ascontiguousarray(words).view(ml_dtypes.float8_e4m3fn).astype(np.float64) * np.repeat(np.exp2(scales.astype(np.float64) - 127.0), 8, axis=1)[..., None]
    return vals.transpose(0, 1, 3, 2).reshape(g * 512, n)

def planes(y):
    n, m = y.shape
    v = y.astype(np.float32).astype(ml_dtypes.bfloat16).astype(np.float64).reshape(n // 32, 32, m)
    top = np.abs(v).max(1)
    byte = np.clip(np.where(top > 0, np.frexp(top)[1] - 1 + 127 - 7, 1), 1, 254)
    codes = (v * np.exp2(127.0 - byte)[:, None, :]).reshape(n, m).astype(np.float32).astype(ml_dtypes.float8_e4m3fn).view(np.uint8)
    words = codes.reshape(n // 512, 128, 4, m).transpose(0, 1, 3, 2)
    return np.ascontiguousarray(words), np.ascontiguousarray(byte.astype(np.uint8).reshape(n // 512, 16, m))


K, T, S, V, H = 512, 2048, 512, 512, 512


def setup_inputs():
    n = np.random.standard_normal
    s = mx_kscale(K)[:, None]
    u = mx_kscale(S)
    packed_xT = pack_weight(n((K, T)) * s)
    packed_w1 = pack_weight(n((K, H)) / np.sqrt(K) / s)
    packed_w2 = pack_weight(n((K, H)) / np.sqrt(K) / s)
    return {
        "x_words": packed_xT[0],
        "x_scales": packed_xT[1],
        "w1_words": packed_w1[0],
        "w1_scales": packed_w1[1],
        "w2_words": packed_w2[0],
        "w2_scales": packed_w2[1],
        "ga": (np.random.uniform(0.5, 1.5, (H, 1)) * u[:, None]).astype(np.float32),
        "gb": (np.random.uniform(0.5, 1.5, (H, 1)) / u[:, None]).astype(np.float32),
        "offs": striped(np.random.permutation(T)[:S]),
        "two": striped(np.random.permutation(T)[:V]),
        "n1": striped8(np.stack([np.random.permutation(S) for _ in range(8)])),
        "nq": striped8(np.stack([np.random.permutation(V) for _ in range(8)])),
        "cq": striped8(np.stack([np.random.permutation(V) for _ in range(8)])),
    }


def reference(x_words, x_scales, w1_words, w1_scales, w2_words, w2_scales, ga, gb, offs, two, n1, nq, cq):
    xq = unpack_weight(x_words, x_scales)[:, unstriped(offs)]
    a = unpack_weight(w1_words, w1_scales).T @ xq
    z = f64(ga) * ((a - (a[np.arange(H)[:, None], runs(n1, H)])) ** 2)
    x_two = unpack_weight(x_words, x_scales)[:, unstriped(two)]
    b = unpack_weight(w2_words, w2_scales).T @ x_two
    z2 = f64(gb) * (np.tanh(b[np.arange(H)[:, None], runs(nq, H)]))
    s = 0.0625 * ((mxq(z, 0, "e4m3").T @ mxq(z2, 0, "e4m3")))
    out_0 = np.maximum(s, s[np.arange(S)[:, None], runs(cq, S)])
    return (out_0,) + planes(out_0)

@@ -1,0 +1,233 @@
+from contextlib import ExitStack
+
+import concourse.mybir as mybir
+
+K, T, S, V, H = 512, 2048, 512, 512, 512
+FLOPS = 3 * 2 * 512 * 512 * 512
+
+F32 = mybir.dt.float32
+BF16 = mybir.dt.bfloat16
+I32 = mybir.dt.int32
+U32 = mybir.dt.uint32
+U16 = mybir.dt.uint16
+U8 = mybir.dt.uint8
+FP8X4 = mybir.dt.float8_e4m3fn_x4
+ALU = mybir.AluOpType
+ACT = mybir.ActivationFunctionType
+
+P = 128
+PACK = 4
+HALF = 256
+HALVES = [slice(0, HALF), slice(HALF, 2 * HALF)]
+OUT_CHUNKS = [slice(0, 256), slice(256, 384), slice(384, 512)]
+
+
+def entries(offsets, cols):
+    return offsets[:, cols.start // 16 : cols.stop // 16]
+
+
+def as_words(dram):
+    return dram[0].rearrange("p c r -> p (c r)").bitcast(I32)
+
+
+def load_scale_rows(queue, plane, first, dram):
+    for q in range(4):
+        queue.dma_start(
+            out=plane[32 * q + first : 32 * q + first + 4, :].bitcast(I32),
+            in_=dram[0, 4 * q : 4 * q + 4, :].bitcast(I32),
+        )
+
+
+def deal(engine, out, in_, run):
+    engine.tensor_copy(
+        out=out.rearrange("p (t c i) -> p c t i", t=PACK, i=run),
+        in_=in_.rearrange("p (c i t) -> p c t i", t=PACK, i=run),
+    )
+
+
+def interleaved(dst, src):
+    return (
+        dst.rearrange("p (c i) t -> p c t i", i=4),
+        src.rearrange("p t (c i) -> p c t i", i=4),
+    )
+
+
+def tile_picked_keysq_none_po_kernel(
+    tc, x_words, x_scales, w1_words, w1_scales, w2_words, w2_scales, ga, gb, offs, two, n1, nq, cq, out_0, out_1, out_2
+):
+    nc = tc.nc
+    with ExitStack() as ctx:
+        keep = ctx.enter_context(tc.tile_pool(name="keep", bufs=1))
+        psum = ctx.enter_context(tc.psum_pool(name="psum", bufs=1))
+
+        def list_tile(name, dram):
+            tile = keep.tile([P, 32], U16, name=name)
+            nc.sync.dma_start(tile[:], dram)
+            return tile
+
+        xs = keep.tile([P, T], U8, align_bytes=64)
+        ws = keep.tile([P, H], U8, align_bytes=64)
+        nc.vector.memset(xs[:].bitcast(I32), 0)
+        nc.vector.memset(ws[:].bitcast(I32), 0)
+
+        offs_t = list_tile("offs_t", offs)
+        two_t = list_tile("two_t", two)
+        load_scale_rows(nc.sync, xs, 0, x_scales)
+        xw = keep.tile([P, T], I32, align_bytes=64)
+        nc.sync.dma_start(out=xw[:], in_=as_words(x_words))
+        w1 = keep.tile([P, H], I32, align_bytes=64)
+        nc.sync.dma_start(out=w1[:], in_=as_words(w1_words))
+        load_scale_rows(nc.sync, ws, 0, w1_scales)
+        ga_t = keep.tile([P, PACK], F32)
+        gb_t = keep.tile([P, PACK], F32)
+        nc.gpsimd.dma_start(out=ga_t[:], in_=ga.rearrange("(p t) o -> p (t o)", t=PACK))
+        load_scale_rows(nc.gpsimd, ws, 4, w2_scales)
+        nc.sync.dma_start(out=gb_t[:], in_=gb.rearrange("(p t) o -> p (t o)", t=PACK))
+        w2 = keep.tile([P, H], I32, align_bytes=64)
+        nc.sync.dma_start(out=w2[:], in_=as_words(w2_words))
+        n1_t = list_tile("n1_t", n1)
+        nq_t = list_tile("nq_t", nq)
+        cq_t = list_tile("cq_t", cq)
+
+        one_half = keep.tile([P, PACK], F32)
+        nc.gpsimd.memset(one_half[:], 0.5)
+        step = keep.tile([P, PACK], F32)
+        sign = keep.tile([P, PACK], F32)
+        ga_abs = keep.tile([P, PACK], F32)
+        ga_root = keep.tile([P, PACK], F32)
+        gb_signed = keep.tile([P, PACK], F32)
+        nc.gpsimd.tensor_scalar(step[:], ga_t[:], 0.0, 2.0, ALU.is_ge, ALU.mult)
+        nc.gpsimd.tensor_scalar(sign[:], step[:], -1.0, 1.0, ALU.add, ALU.mult)
+        nc.gpsimd.tensor_tensor(ga_abs[:], ga_t[:], sign[:], ALU.mult)
+        nc.gpsimd.tensor_tensor(ga_root[:], ga_abs[:], one_half[:], ALU.pow)
+        nc.gpsimd.tensor_tensor(gb_signed[:], gb_t[:], sign[:], ALU.mult)
+        gb_wide = keep.tile([P, PACK, HALF], F32)
+        nc.scalar.activation(gb_wide[:], gb_signed[:].unsqueeze(2).to_broadcast([P, PACK, HALF]), ACT.Copy)
+
+        xa_s = keep.tile([P, S], U8, align_bytes=64)
+        xb_s = keep.tile([P, V], U8, align_bytes=64)
+        xa_w = keep.tile([P, S], U32, align_bytes=64)
+        xb_w = keep.tile([P, V], U32, align_bytes=64)
+        w1_d = keep.tile([P, H], U32, align_bytes=64)
+        w2_d = keep.tile([P, H], U32, align_bytes=64)
+        ws_d = keep.tile([P, H], U8, align_bytes=64)
+        nc.vector.tensor_copy(xa_s[:], xs[:].indirect(offs_t[:]))
+        nc.vector.tensor_copy(xb_s[:], xs[:].indirect(two_t[:]))
+        nc.vector.tensor_copy(xa_w[:], xw[:].bitcast(U32).indirect(offs_t[:]))
+        deal(nc.vector, w1_d[:], w1[:].bitcast(U32), 4)
+        deal(nc.vector, ws_d[:], ws[:], 16)
+
+        def project(bank, w_d, first, x_w, x_s, t):
+            cols = slice(P * t, P * (t + 1))
+            nc.tensor.matmul_mx(
+                out=bank[:],
+                lhsT=w_d[:, cols].bitcast(FP8X4),
+                lhsT_scale=ws_d[first:P, cols],
+                rhs=x_w[:].bitcast(FP8X4),
+                rhs_scale=x_s[:],
+                start=True,
+                stop=True,
+            )
+
+        a_win = [keep.tile([P, S], F32, name="a_win%d" % t) for t in range(PACK)]
+        a_own = [keep.tile([P, S], F32, name="a_own%d" % t) for t in range(PACK)]
+        for t in range(PACK):
+            bank = psum.tile([P, S], F32, name="low%d" % t)
+            project(bank, w1_d, 0, xa_w, xa_s, t)
+            nc.scalar.activation(a_win[t][:], bank[:], ACT.Copy, scale=ga_root[:, t : t + 1])
+            nc.scalar.activation(a_own[t][:], bank[:], ACT.Copy, scale=ga_root[:, t : t + 1])
+
+        nc.vector.tensor_copy(xb_w[:], xw[:].bitcast(U32).indirect(two_t[:]))
+        deal(nc.vector, w2_d[:], w2[:].bitcast(U32), 4)
+        b_win = [keep.tile([P, V], F32, name="b_win%d" % t) for t in range(PACK)]
+        for t in range(PACK):
+            bank = psum.tile([P, V], F32, name="high%d" % t)
+            project(bank, w2_d, 4, xb_w, xb_s, t)
+            nc.scalar.activation(b_win[t][:], bank[:], ACT.Tanh)
+
+        diff = keep.tile([P, PACK, S], F32)
+        for t in range(PACK):
+            for cols in HALVES:
+                nc.vector.tensor_tensor(
+                    diff[:, t, cols], a_win[t][:].indirect(entries(n1_t, cols)), a_own[t][:, cols], ALU.subtract
+                )
+        z = keep.tile([P, PACK, P, PACK], BF16, align_bytes=64)
+        nc.scalar.activation(
+            z[:].rearrange("p u m t -> p m t u"),
+            diff[:].rearrange("p t (m u) -> p m t u", u=PACK),
+            ACT.Square,
+        )
+
+        z2_f = [keep.tile([P, PACK, HALF], F32, name="z2_f%d" % h) for h in range(2)]
+        z2 = [keep.tile([P, HALF, PACK], BF16, name="z2_%d" % h, align_bytes=64) for h in range(2)]
+        z2_w = [keep.tile([P, HALF], U32, name="z2_w%d" % h, align_bytes=64) for h in range(2)]
+        z2_s = [keep.tile([P, HALF], U8, name="z2_s%d" % h, align_bytes=64) for h in range(2)]
+        z_w = keep.tile([P, S], U32, align_bytes=64)
+        z_s = keep.tile([P, S], U8, align_bytes=64)
+        s_win = [keep.tile([P, V], F32, name="s_win%d" % t) for t in range(PACK)]
+
+        for h, cols in enumerate(HALVES):
+            for t in range(PACK):
+                nc.vector.tensor_tensor(
+                    z2_f[h][:, t, :], b_win[t][:].indirect(entries(nq_t, cols)), gb_wide[:, t, :], ALU.mult
+                )
+        dst, src = interleaved(z2[0][:], z2_f[0][:])
+        nc.scalar.activation(dst, src, ACT.Copy)
+        nc.vector.quantize_mx(out=z_w[:].bitcast(FP8X4), scales=z_s[:], in_=z[:].rearrange("p u m t -> p (u m t)"))
+        dst, src = interleaved(z2[1][:], z2_f[1][:])
+        nc.vector.tensor_copy(dst, src)
+        for h, cols in enumerate(HALVES):
+            nc.vector.quantize_mx(
+                out=z2_w[h][:].bitcast(FP8X4), scales=z2_s[h][:], in_=z2[h][:].rearrange("p c t -> p (c t)")
+            )
+            for t in range(PACK):
+                rows = slice(P * t, P * (t + 1))
+                bank = psum.tile([P, V], F32, name=("low%d", "high%d")[h] % t)
+                nc.tensor.matmul_mx(
+                    out=bank[:, 0:HALF],
+                    lhsT=z_w[:, rows].bitcast(FP8X4),
+                    lhsT_scale=z_s[:, rows],
+                    rhs=z2_w[h][:].bitcast(FP8X4),
+                    rhs_scale=z2_s[h][:],
+                    start=True,
+                    stop=True,
+                )
+                nc.scalar.activation(s_win[t][:, cols], bank[:, 0:HALF], ACT.Copy, scale=0.0625)
+
+        out_rows = out_0.rearrange("(p t) v -> p t v", t=PACK)
+        out_words = as_words(out_1)
+        o_s = keep.tile([P, V], U8, align_bytes=64)
+        pending = []
+
+        def hand_on(cols, o_b, o_w, queue):
+            nc.vector.quantize_mx(
+                out=o_w[:].bitcast(FP8X4), scales=o_s[:, cols], in_=o_b[:].rearrange("p c t -> p (c t)")
+            )
+            queue.dma_start(out=out_words[:, cols], in_=o_w[:].bitcast(I32))
+
+        for c, cols in enumerate(OUT_CHUNKS):
+            width = cols.stop - cols.start
+            last = c == len(OUT_CHUNKS) - 1
+            other = keep.tile([P, PACK, width], F32, name="other%d" % c)
+            o_f = keep.tile([P, PACK, width], F32, name="o_f%d" % c)
+            o_b = keep.tile([P, width, PACK], BF16, name="o_b%d" % c, align_bytes=64)
+            o_w = keep.tile([P, width], U32, name="o_w%d" % c, align_bytes=64)
+            for t in range(PACK + 1):
+                if t < PACK:
+                    nc.vector.tensor_copy(other[:, t, :], s_win[t][:].indirect(entries(cq_t, cols)))
+                if t > 0:
+                    nc.vector.tensor_tensor(o_f[:, t - 1, :], other[:, t - 1, :], s_win[t - 1][:, cols], ALU.max)
+            nc.sync.dma_start(out=out_rows[:, :, cols], in_=o_f[:])
+            for args in pending:
+                hand_on(*args)
+            dst, src = interleaved(o_b[:], o_f[:])
+            if last:
+                nc.vector.tensor_copy(dst, src)
+                hand_on(cols, o_b, o_w, nc.scalar)
+            else:
+                nc.scalar.activation(dst, src, ACT.Copy)
+            pending = [(cols, o_b, o_w, nc.sync)]
+        for q in range(4):
+            (nc.sync, nc.scalar)[q % 2].dma_start(
+                out=out_2[0, 4 * q : 4 * q + 4, :].bitcast(I32), in_=o_s[32 * q : 32 * q + 4, :].bitcast(I32)
+            )

@@ -26,14 +26,18 @@ def entries(offsets, cols):
     return offsets[:, cols.start // 16 : cols.stop // 16]
 
 
+def window(tile, offsets):
+    return tile[:].rearrange("p h c -> p (h c)").indirect(offsets[:])
+
+
 def as_words(dram):
     return dram[0].rearrange("p c r -> p (c r)").bitcast(I32)
 
 
-def load_scale_rows(queue, plane, first, dram):
+def load_scale_rows(queue, plane, dram):
     for q in range(4):
         queue.dma_start(
-            out=plane[32 * q + first : 32 * q + first + 4, :].bitcast(I32),
+            out=plane[32 * q : 32 * q + 4, :].bitcast(I32),
             in_=dram[0, 4 * q : 4 * q + 4, :].bitcast(I32),
         )
 
@@ -66,91 +70,89 @@ def tile_picked_keysq_none_po_kernel(
             return tile
 
         xs = keep.tile([P, T], U8, align_bytes=64)
-        ws = keep.tile([P, H], U8, align_bytes=64)
+        w1_s = keep.tile([P, H], U8, align_bytes=64)
+        w2_s = keep.tile([P, H], U8, align_bytes=64, tag="early")
         nc.vector.memset(xs[:].bitcast(I32), 0)
-        nc.vector.memset(ws[:].bitcast(I32), 0)
+        nc.vector.memset(w1_s[:].bitcast(I32), 0)
+        nc.vector.memset(w2_s[:].bitcast(I32), 0)
 
         offs_t = list_tile("offs_t", offs)
         two_t = list_tile("two_t", two)
-        load_scale_rows(nc.sync, xs, 0, x_scales)
-        xw = keep.tile([P, T], I32, align_bytes=64)
-        nc.sync.dma_start(out=xw[:], in_=as_words(x_words))
-        w1 = keep.tile([P, H], I32, align_bytes=64)
-        nc.sync.dma_start(out=w1[:], in_=as_words(w1_words))
-        load_scale_rows(nc.sync, ws, 0, w1_scales)
         ga_t = keep.tile([P, PACK], F32)
         gb_t = keep.tile([P, PACK], F32)
-        nc.gpsimd.dma_start(out=ga_t[:], in_=ga.rearrange("(p t) o -> p (t o)", t=PACK))
-        load_scale_rows(nc.gpsimd, ws, 4, w2_scales)
-        nc.sync.dma_start(out=gb_t[:], in_=gb.rearrange("(p t) o -> p (t o)", t=PACK))
+        nc.sync.dma_start(out=ga_t[:], in_=ga.rearrange("(p t) o -> p (t o)", t=PACK))
+        nc.gpsimd.dma_start(out=gb_t[:], in_=gb.rearrange("(p t) o -> p (t o)", t=PACK))
+        load_scale_rows(nc.sync, xs, x_scales)
+        xw = keep.tile([P, T], I32, align_bytes=64)
+        nc.sync.dma_start(out=xw[:], in_=as_words(x_words))
+        load_scale_rows(nc.sync, w1_s, w1_scales)
+        w1 = keep.tile([P, H], I32, align_bytes=64, tag="words")
+        nc.sync.dma_start(out=w1[:], in_=as_words(w1_words))
+        n1_t = list_tile("n1_t", n1)
         w2 = keep.tile([P, H], I32, align_bytes=64)
         nc.sync.dma_start(out=w2[:], in_=as_words(w2_words))
-        n1_t = list_tile("n1_t", n1)
+        load_scale_rows(nc.sync, w2_s, w2_scales)
         nq_t = list_tile("nq_t", nq)
         cq_t = list_tile("cq_t", cq)
 
         one_half = keep.tile([P, PACK], F32)
         nc.gpsimd.memset(one_half[:], 0.5)
-        step = keep.tile([P, PACK], F32)
         sign = keep.tile([P, PACK], F32)
         ga_abs = keep.tile([P, PACK], F32)
         ga_root = keep.tile([P, PACK], F32)
-        gb_signed = keep.tile([P, PACK], F32)
-        nc.gpsimd.tensor_scalar(step[:], ga_t[:], 0.0, 2.0, ALU.is_ge, ALU.mult)
-        nc.gpsimd.tensor_scalar(sign[:], step[:], -1.0, 1.0, ALU.add, ALU.mult)
-        nc.gpsimd.tensor_tensor(ga_abs[:], ga_t[:], sign[:], ALU.mult)
+        nc.scalar.activation(ga_abs[:], ga_t[:], ACT.Abs)
+        nc.scalar.activation(sign[:], ga_t[:], ACT.Sign)
         nc.gpsimd.tensor_tensor(ga_root[:], ga_abs[:], one_half[:], ALU.pow)
-        nc.gpsimd.tensor_tensor(gb_signed[:], gb_t[:], sign[:], ALU.mult)
-        gb_wide = keep.tile([P, PACK, HALF], F32)
-        nc.scalar.activation(gb_wide[:], gb_signed[:].unsqueeze(2).to_broadcast([P, PACK, HALF]), ACT.Copy)
+        a_win = [keep.tile([P, 2, S], F32, name="a_win%d" % t) for t in range(PACK)]
+        b_win = [keep.tile([P, 2, V], F32, name="b_win%d" % t) for t in range(PACK)]
+        for t in range(PACK):
+            nc.scalar.activation(
+                a_win[t][:, 1, :], gb_t[:, t : t + 1].to_broadcast([P, V]), ACT.Copy, scale=sign[:, t : t + 1]
+            )
 
         xa_s = keep.tile([P, S], U8, align_bytes=64)
         xb_s = keep.tile([P, V], U8, align_bytes=64)
         xa_w = keep.tile([P, S], U32, align_bytes=64)
-        xb_w = keep.tile([P, V], U32, align_bytes=64)
         w1_d = keep.tile([P, H], U32, align_bytes=64)
         w2_d = keep.tile([P, H], U32, align_bytes=64)
-        ws_d = keep.tile([P, H], U8, align_bytes=64)
+        w1_sd = keep.tile([P, H], U8, align_bytes=64)
+        w2_sd = keep.tile([P, H], U8, align_bytes=64)
         nc.vector.tensor_copy(xa_s[:], xs[:].indirect(offs_t[:]))
         nc.vector.tensor_copy(xb_s[:], xs[:].indirect(two_t[:]))
         nc.vector.tensor_copy(xa_w[:], xw[:].bitcast(U32).indirect(offs_t[:]))
+        deal(nc.vector, w1_sd[:], w1_s[:], 16)
         deal(nc.vector, w1_d[:], w1[:].bitcast(U32), 4)
-        deal(nc.vector, ws_d[:], ws[:], 16)
 
-        def project(bank, w_d, first, x_w, x_s, t):
+        def project(bank, w_d, w_sd, x_w, x_s, t):
             cols = slice(P * t, P * (t + 1))
             nc.tensor.matmul_mx(
                 out=bank[:],
                 lhsT=w_d[:, cols].bitcast(FP8X4),
-                lhsT_scale=ws_d[first:P, cols],
+                lhsT_scale=w_sd[:, cols],
                 rhs=x_w[:].bitcast(FP8X4),
                 rhs_scale=x_s[:],
                 start=True,
                 stop=True,
             )
 
-        a_win = [keep.tile([P, S], F32, name="a_win%d" % t) for t in range(PACK)]
-        a_own = [keep.tile([P, S], F32, name="a_own%d" % t) for t in range(PACK)]
         for t in range(PACK):
             bank = psum.tile([P, S], F32, name="low%d" % t)
-            project(bank, w1_d, 0, xa_w, xa_s, t)
-            nc.scalar.activation(a_win[t][:], bank[:], ACT.Copy, scale=ga_root[:, t : t + 1])
-            nc.scalar.activation(a_own[t][:], bank[:], ACT.Copy, scale=ga_root[:, t : t + 1])
+            project(bank, w1_d, w1_sd, xa_w, xa_s, t)
+            nc.scalar.activation(a_win[t][:, 0, :], bank[:], ACT.Copy, scale=ga_root[:, t : t + 1])
+            nc.scalar.activation(b_win[t][:, 1, :], bank[:], ACT.Copy, scale=ga_root[:, t : t + 1])
 
+        xb_w = keep.tile([P, V], U32, align_bytes=64, tag="words")
         nc.vector.tensor_copy(xb_w[:], xw[:].bitcast(U32).indirect(two_t[:]))
         deal(nc.vector, w2_d[:], w2[:].bitcast(U32), 4)
-        b_win = [keep.tile([P, V], F32, name="b_win%d" % t) for t in range(PACK)]
+        deal(nc.vector, w2_sd[:], w2_s[:], 16)
         for t in range(PACK):
             bank = psum.tile([P, V], F32, name="high%d" % t)
-            project(bank, w2_d, 4, xb_w, xb_s, t)
-            nc.scalar.activation(b_win[t][:], bank[:], ACT.Tanh)
+            project(bank, w2_d, w2_sd, xb_w, xb_s, t)
+            nc.scalar.activation(b_win[t][:, 0, :], bank[:], ACT.Tanh)
 
-        diff = keep.tile([P, PACK, S], F32)
+        diff = keep.tile([P, PACK, S], F32, align_bytes=64, tag="early")
         for t in range(PACK):
-            for cols in HALVES:
-                nc.vector.tensor_tensor(
-                    diff[:, t, cols], a_win[t][:].indirect(entries(n1_t, cols)), a_own[t][:, cols], ALU.subtract
-                )
+            nc.vector.tensor_tensor(diff[:, t, :], window(a_win[t], n1_t), b_win[t][:, 1, :], ALU.subtract)
         z = keep.tile([P, PACK, P, PACK], BF16, align_bytes=64)
         nc.scalar.activation(
             z[:].rearrange("p u m t -> p m t u"),
@@ -158,7 +160,7 @@ def tile_picked_keysq_none_po_kernel(
             ACT.Square,
         )
 
-        z2_f = [keep.tile([P, PACK, HALF], F32, name="z2_f%d" % h) for h in range(2)]
+        z2_f = keep.tile([P, PACK, V], F32)
         z2 = [keep.tile([P, HALF, PACK], BF16, name="z2_%d" % h, align_bytes=64) for h in range(2)]
         z2_w = [keep.tile([P, HALF], U32, name="z2_w%d" % h, align_bytes=64) for h in range(2)]
         z2_s = [keep.tile([P, HALF], U8, name="z2_s%d" % h, align_bytes=64) for h in range(2)]
@@ -166,21 +168,19 @@ def tile_picked_keysq_none_po_kernel(
         z_s = keep.tile([P, S], U8, align_bytes=64)
         s_win = [keep.tile([P, V], F32, name="s_win%d" % t) for t in range(PACK)]
 
-        for h, cols in enumerate(HALVES):
-            for t in range(PACK):
-                nc.vector.tensor_tensor(
-                    z2_f[h][:, t, :], b_win[t][:].indirect(entries(nq_t, cols)), gb_wide[:, t, :], ALU.mult
-                )
-        dst, src = interleaved(z2[0][:], z2_f[0][:])
+        for t in range(PACK):
+            nc.vector.tensor_tensor(z2_f[:, t, :], window(b_win[t], nq_t), a_win[t][:, 1, :], ALU.mult)
+        dst, src = interleaved(z2[1][:], z2_f[:, :, HALVES[1]])
         nc.scalar.activation(dst, src, ACT.Copy)
-        nc.vector.quantize_mx(out=z_w[:].bitcast(FP8X4), scales=z_s[:], in_=z[:].rearrange("p u m t -> p (u m t)"))
-        dst, src = interleaved(z2[1][:], z2_f[1][:])
+        dst, src = interleaved(z2[0][:], z2_f[:, :, HALVES[0]])
         nc.vector.tensor_copy(dst, src)
+        nc.vector.quantize_mx(out=z_w[:].bitcast(FP8X4), scales=z_s[:], in_=z[:].rearrange("p u m t -> p (u m t)"))
         for h, cols in enumerate(HALVES):
             nc.vector.quantize_mx(
                 out=z2_w[h][:].bitcast(FP8X4), scales=z2_s[h][:], in_=z2[h][:].rearrange("p c t -> p (c t)")
             )
-            for t in range(PACK):
+        for t in range(PACK):
+            for h, cols in enumerate(HALVES):
                 rows = slice(P * t, P * (t + 1))
                 bank = psum.tile([P, V], F32, name=("low%d", "high%d")[h] % t)
                 nc.tensor.matmul_mx(
@@ -208,15 +208,16 @@ def tile_picked_keysq_none_po_kernel(
         for c, cols in enumerate(OUT_CHUNKS):
             width = cols.stop - cols.start
             last = c == len(OUT_CHUNKS) - 1
-            other = keep.tile([P, PACK, width], F32, name="other%d" % c)
+            other = []
             o_f = keep.tile([P, PACK, width], F32, name="o_f%d" % c)
             o_b = keep.tile([P, width, PACK], BF16, name="o_b%d" % c, align_bytes=64)
             o_w = keep.tile([P, width], U32, name="o_w%d" % c, align_bytes=64)
             for t in range(PACK + 1):
                 if t < PACK:
-                    nc.vector.tensor_copy(other[:, t, :], s_win[t][:].indirect(entries(cq_t, cols)))
+                    other.append(keep.tile([P, width], F32, name="other%d" % ((PACK * c + t) % 3)))
+                    nc.vector.tensor_copy(other[t][:], s_win[t][:].indirect(entries(cq_t, cols)))
                 if t > 0:
-                    nc.vector.tensor_tensor(o_f[:, t - 1, :], other[:, t - 1, :], s_win[t - 1][:, cols], ALU.max)
+                    nc.vector.tensor_tensor(o_f[:, t - 1, :], other[t - 1][:], s_win[t - 1][:, cols], ALU.max)
             nc.sync.dma_start(out=out_rows[:, :, cols], in_=o_f[:])
             for args in pending:
                 hand_on(*args)

@@ -19,7 +19,6 @@ P = 128
 PACK = 4
 HALF = 256
 HALVES = [slice(0, HALF), slice(HALF, 2 * HALF)]
-OUT_CHUNKS = [slice(0, 256), slice(256, 384), slice(384, 512)]
 
 
 def entries(offsets, cols):
@@ -153,42 +152,45 @@ def tile_picked_keysq_none_po_kernel(
         diff = keep.tile([P, PACK, S], F32, align_bytes=64, tag="early")
         for t in range(PACK):
             nc.vector.tensor_tensor(diff[:, t, :], window(a_win[t], n1_t), b_win[t][:, 1, :], ALU.subtract)
-        z = keep.tile([P, PACK, P, PACK], BF16, align_bytes=64)
-        nc.scalar.activation(
-            z[:].rearrange("p u m t -> p m t u"),
-            diff[:].rearrange("p t (m u) -> p m t u", u=PACK),
-            ACT.Square,
-        )
+        z = [keep.tile([P, 2, P, PACK], BF16, name="z%d" % g, align_bytes=64) for g in range(2)]
+        for g in range(2):
+            nc.scalar.activation(
+                z[g][:].rearrange("p u m t -> p m t u"),
+                diff[:].rearrange("p t (m u) -> p m t u", u=PACK)[:, :, :, 2 * g : 2 * g + 2],
+                ACT.Square,
+            )
 
         z2_f = keep.tile([P, PACK, V], F32)
-        z2 = [keep.tile([P, HALF, PACK], BF16, name="z2_%d" % h, align_bytes=64) for h in range(2)]
-        z2_w = [keep.tile([P, HALF], U32, name="z2_w%d" % h, align_bytes=64) for h in range(2)]
-        z2_s = [keep.tile([P, HALF], U8, name="z2_s%d" % h, align_bytes=64) for h in range(2)]
-        z_w = keep.tile([P, S], U32, align_bytes=64)
-        z_s = keep.tile([P, S], U8, align_bytes=64)
-        s_win = [keep.tile([P, V], F32, name="s_win%d" % t) for t in range(PACK)]
-
         for t in range(PACK):
             nc.vector.tensor_tensor(z2_f[:, t, :], window(b_win[t], nq_t), a_win[t][:, 1, :], ALU.mult)
+        z2 = [keep.tile([P, HALF, PACK], BF16, name="z2_%d" % h, align_bytes=64) for h in range(2)]
         dst, src = interleaved(z2[1][:], z2_f[:, :, HALVES[1]])
         nc.scalar.activation(dst, src, ACT.Copy)
         dst, src = interleaved(z2[0][:], z2_f[:, :, HALVES[0]])
         nc.vector.tensor_copy(dst, src)
-        nc.vector.quantize_mx(out=z_w[:].bitcast(FP8X4), scales=z_s[:], in_=z[:].rearrange("p u m t -> p (u m t)"))
-        for h, cols in enumerate(HALVES):
-            nc.vector.quantize_mx(
-                out=z2_w[h][:].bitcast(FP8X4), scales=z2_s[h][:], in_=z2[h][:].rearrange("p c t -> p (c t)")
-            )
+
+        def quantise(name, values, tag):
+            words = keep.tile([P, HALF], U32, name=name + "_w", tag=tag, align_bytes=64)
+            scales = keep.tile([P, HALF], U8, name=name + "_s", align_bytes=64)
+            nc.vector.quantize_mx(out=words[:].bitcast(FP8X4), scales=scales[:], in_=values)
+            return words, scales
+
+        z_q = [quantise("zq0", z[0][:].rearrange("p u m t -> p (u m t)"), "zq0")]
+        z2_q = [quantise("z2q0", z2[0][:].rearrange("p c t -> p (c t)"), "z0")]
+        z2_q.append(quantise("z2q1", z2[1][:].rearrange("p c t -> p (c t)"), "z2q1"))
+        z_q.append(quantise("zq1", z[1][:].rearrange("p u m t -> p (u m t)"), "z2_1"))
+
+        s_win = [keep.tile([P, V], F32, name="s_win%d" % t) for t in range(PACK)]
         for t in range(PACK):
+            rows = slice(P * (t % 2), P * (t % 2 + 1))
             for h, cols in enumerate(HALVES):
-                rows = slice(P * t, P * (t + 1))
                 bank = psum.tile([P, V], F32, name=("low%d", "high%d")[h] % t)
                 nc.tensor.matmul_mx(
                     out=bank[:, 0:HALF],
-                    lhsT=z_w[:, rows].bitcast(FP8X4),
-                    lhsT_scale=z_s[:, rows],
-                    rhs=z2_w[h][:].bitcast(FP8X4),
-                    rhs_scale=z2_s[h][:],
+                    lhsT=z_q[t // 2][0][:, rows].bitcast(FP8X4),
+                    lhsT_scale=z_q[t // 2][1][:, rows],
+                    rhs=z2_q[h][0][:].bitcast(FP8X4),
+                    rhs_scale=z2_q[h][1][:],
                     start=True,
                     stop=True,
                 )
@@ -197,37 +199,39 @@ def tile_picked_keysq_none_po_kernel(
         out_rows = out_0.rearrange("(p t) v -> p t v", t=PACK)
         out_words = as_words(out_1)
         o_s = keep.tile([P, V], U8, align_bytes=64)
-        pending = []
+        o_b = [keep.tile([P, HALF, PACK], BF16, name="o_b%d" % h, align_bytes=64) for h in range(2)]
 
-        def hand_on(cols, o_b, o_w, queue):
-            nc.vector.quantize_mx(
-                out=o_w[:].bitcast(FP8X4), scales=o_s[:, cols], in_=o_b[:].rearrange("p c t -> p (c t)")
-            )
-            queue.dma_start(out=out_words[:, cols], in_=o_w[:].bitcast(I32))
-
-        for c, cols in enumerate(OUT_CHUNKS):
+        def larger(cols, tags, before_last):
             width = cols.stop - cols.start
-            last = c == len(OUT_CHUNKS) - 1
+            o_f = keep.tile([P, PACK, width], F32, name="o_f%d" % cols.start)
             other = []
-            o_f = keep.tile([P, PACK, width], F32, name="o_f%d" % c)
-            o_b = keep.tile([P, width, PACK], BF16, name="o_b%d" % c, align_bytes=64)
-            o_w = keep.tile([P, width], U32, name="o_w%d" % c, align_bytes=64)
             for t in range(PACK + 1):
+                if t == PACK - 1:
+                    before_last()
                 if t < PACK:
-                    other.append(keep.tile([P, width], F32, name="other%d" % ((PACK * c + t) % 3)))
+                    other.append(keep.tile([P, width], F32, name="other", tag=tags[t], align_bytes=64))
                     nc.vector.tensor_copy(other[t][:], s_win[t][:].indirect(entries(cq_t, cols)))
                 if t > 0:
                     nc.vector.tensor_tensor(o_f[:, t - 1, :], other[t - 1][:], s_win[t - 1][:, cols], ALU.max)
             nc.sync.dma_start(out=out_rows[:, :, cols], in_=o_f[:])
-            for args in pending:
-                hand_on(*args)
-            dst, src = interleaved(o_b[:], o_f[:])
-            if last:
-                nc.vector.tensor_copy(dst, src)
-                hand_on(cols, o_b, o_w, nc.scalar)
-            else:
-                nc.scalar.activation(dst, src, ACT.Copy)
-            pending = [(cols, o_b, o_w, nc.sync)]
+            return o_f
+
+        def hand_on(h, queue):
+            o_w = keep.tile([P, HALF], U32, name="o_w%d" % h, align_bytes=64)
+            nc.vector.quantize_mx(
+                out=o_w[:].bitcast(FP8X4), scales=o_s[:, HALVES[h]], in_=o_b[h][:].rearrange("p c t -> p (c t)")
+            )
+            queue.dma_start(out=out_words[:, HALVES[h]], in_=o_w[:].bitcast(I32))
+
+        first = larger(slice(0, 384), ["ring0", "ring1", "ring2", "ring0"], lambda: None)
+        dst, src = interleaved(o_b[0][:], first[:, :, 0:256])
+        nc.scalar.activation(dst, src, ACT.Copy)
+        dst, src = interleaved(o_b[1][:, 0:128, :], first[:, :, 256:384])
+        nc.scalar.activation(dst, src, ACT.Copy)
+        last = larger(slice(384, 512), ["ring1", "ring2", "ring0", "o_b0"], lambda: hand_on(0, nc.sync))
+        dst, src = interleaved(o_b[1][:, 128:256, :], last[:])
+        nc.vector.tensor_copy(dst, src)
+        hand_on(1, nc.scalar)
         for q in range(4):
             (nc.sync, nc.scalar)[q % 2].dma_start(
                 out=out_2[0, 4 * q : 4 * q + 4, :].bitcast(I32), in_=o_s[32 * q : 32 * q + 4, :].bitcast(I32)

@@ -34,11 +34,8 @@ def as_words(dram):
 
 
 def load_scale_rows(queue, plane, dram):
-    for q in range(4):
-        queue.dma_start(
-            out=plane[32 * q : 32 * q + 4, :].bitcast(I32),
-            in_=dram[0, 4 * q : 4 * q + 4, :].bitcast(I32),
-        )
+    for r in range(4):
+        queue.dma_start(out=plane[r:P:32, :].bitcast(I32), in_=dram[0, r:16:4, :].bitcast(I32))
 
 
 def deal(engine, out, in_, run):
@@ -50,8 +47,8 @@ def deal(engine, out, in_, run):
 
 def interleaved(dst, src):
     return (
-        dst.rearrange("p (c i) t -> p c t i", i=4),
-        src.rearrange("p t (c i) -> p c t i", i=4),
+        dst.rearrange("p (c i) t -> p c t i", i=2),
+        src.rearrange("p t (c i) -> p c t i", i=2),
     )
 
 
@@ -155,8 +152,8 @@ def tile_picked_keysq_none_po_kernel(
         z = [keep.tile([P, 2, P, PACK], BF16, name="z%d" % g, align_bytes=64) for g in range(2)]
         for g in range(2):
             nc.scalar.activation(
-                z[g][:].rearrange("p u m t -> p m t u"),
-                diff[:].rearrange("p t (m u) -> p m t u", u=PACK)[:, :, :, 2 * g : 2 * g + 2],
+                z[g][:].rearrange("p u m t -> p m u t"),
+                diff[:].rearrange("p t (m u) -> p m u t", u=PACK)[:, :, 2 * g : 2 * g + 2, :],
                 ACT.Square,
             )
 
@@ -199,40 +196,42 @@ def tile_picked_keysq_none_po_kernel(
         out_rows = out_0.rearrange("(p t) v -> p t v", t=PACK)
         out_words = as_words(out_1)
         o_s = keep.tile([P, V], U8, align_bytes=64)
-        o_b = [keep.tile([P, HALF, PACK], BF16, name="o_b%d" % h, align_bytes=64) for h in range(2)]
 
-        def larger(cols, tags, before_last):
+        def larger(cols, ring):
             width = cols.stop - cols.start
             o_f = keep.tile([P, PACK, width], F32, name="o_f%d" % cols.start)
             other = []
             for t in range(PACK + 1):
-                if t == PACK - 1:
-                    before_last()
                 if t < PACK:
-                    other.append(keep.tile([P, width], F32, name="other", tag=tags[t], align_bytes=64))
+                    other.append(keep.tile([P, width], F32, name="other%d" % ((ring + t) % 3)))
                     nc.vector.tensor_copy(other[t][:], s_win[t][:].indirect(entries(cq_t, cols)))
                 if t > 0:
                     nc.vector.tensor_tensor(o_f[:, t - 1, :], other[t - 1][:], s_win[t - 1][:, cols], ALU.max)
             nc.sync.dma_start(out=out_rows[:, :, cols], in_=o_f[:])
             return o_f
 
-        def hand_on(h, queue):
-            o_w = keep.tile([P, HALF], U32, name="o_w%d" % h, align_bytes=64)
+        def hand_on(o_b, cols, tag, queue):
+            o_w = keep.tile([P, cols.stop - cols.start], U32, name="o_w", tag=tag, align_bytes=64)
             nc.vector.quantize_mx(
-                out=o_w[:].bitcast(FP8X4), scales=o_s[:, HALVES[h]], in_=o_b[h][:].rearrange("p c t -> p (c t)")
+                out=o_w[:].bitcast(FP8X4), scales=o_s[:, cols], in_=o_b[:].rearrange("p c t -> p (c t)")
             )
-            queue.dma_start(out=out_words[:, HALVES[h]], in_=o_w[:].bitcast(I32))
+            queue.dma_start(out=out_words[:, cols], in_=o_w[:].bitcast(I32))
 
-        first = larger(slice(0, 384), ["ring0", "ring1", "ring2", "ring0"], lambda: None)
-        dst, src = interleaved(o_b[0][:], first[:, :, 0:256])
+        first = larger(slice(0, 384), 0)
+        o_b0 = keep.tile([P, 256, PACK], BF16, align_bytes=64)
+        o_b1 = keep.tile([P, 128, PACK], BF16, align_bytes=64)
+        dst, src = interleaved(o_b0[:], first[:, :, 0:256])
         nc.scalar.activation(dst, src, ACT.Copy)
-        dst, src = interleaved(o_b[1][:, 0:128, :], first[:, :, 256:384])
+        dst, src = interleaved(o_b1[:], first[:, :, 256:384])
         nc.scalar.activation(dst, src, ACT.Copy)
-        last = larger(slice(384, 512), ["ring1", "ring2", "ring0", "o_b0"], lambda: hand_on(0, nc.sync))
-        dst, src = interleaved(o_b[1][:, 128:256, :], last[:])
+        last = larger(slice(384, 512), 1)
+        hand_on(o_b0, slice(0, 256), "o_w0", nc.sync)
+        o_b2 = keep.tile([P, 128, PACK], BF16, tag="o_b0", align_bytes=64)
+        dst, src = interleaved(o_b2[:], last[:])
         nc.vector.tensor_copy(dst, src)
-        hand_on(1, nc.scalar)
-        for q in range(4):
-            (nc.sync, nc.scalar)[q % 2].dma_start(
-                out=out_2[0, 4 * q : 4 * q + 4, :].bitcast(I32), in_=o_s[32 * q : 32 * q + 4, :].bitcast(I32)
+        hand_on(o_b1, slice(256, 384), "o_w1", nc.sync)
+        hand_on(o_b2, slice(384, 512), "o_b1", nc.scalar)
+        for r in range(4):
+            (nc.sync, nc.scalar)[r % 2].dma_start(
+                out=out_2[0, r:16:4, :].bitcast(I32), in_=o_s[r:P:32, :].bitcast(I32)
             )

@@ -197,7 +197,7 @@ def tile_picked_keysq_none_po_kernel(
         out_words = as_words(out_1)
         o_s = keep.tile([P, V], U8, align_bytes=64)
 
-        def larger(cols, ring):
+        def larger(cols, ring, tiles_a_store):
             width = cols.stop - cols.start
             o_f = keep.tile([P, PACK, width], F32, name="o_f%d" % cols.start)
             other = []
@@ -207,7 +207,9 @@ def tile_picked_keysq_none_po_kernel(
                     nc.vector.tensor_copy(other[t][:], s_win[t][:].indirect(entries(cq_t, cols)))
                 if t > 0:
                     nc.vector.tensor_tensor(o_f[:, t - 1, :], other[t - 1][:], s_win[t - 1][:, cols], ALU.max)
-            nc.sync.dma_start(out=out_rows[:, :, cols], in_=o_f[:])
+                if t > 0 and t % tiles_a_store == 0:
+                    done = slice(t - tiles_a_store, t)
+                    nc.sync.dma_start(out=out_rows[:, done, cols], in_=o_f[:, done, :])
             return o_f
 
         def hand_on(o_b, cols, tag, queue):
@@ -217,14 +219,14 @@ def tile_picked_keysq_none_po_kernel(
             )
             queue.dma_start(out=out_words[:, cols], in_=o_w[:].bitcast(I32))
 
-        first = larger(slice(0, 384), 0)
+        first = larger(slice(0, 384), 0, 1)
         o_b0 = keep.tile([P, 256, PACK], BF16, align_bytes=64)
         o_b1 = keep.tile([P, 128, PACK], BF16, align_bytes=64)
         dst, src = interleaved(o_b0[:], first[:, :, 0:256])
         nc.scalar.activation(dst, src, ACT.Copy)
         dst, src = interleaved(o_b1[:], first[:, :, 256:384])
         nc.scalar.activation(dst, src, ACT.Copy)
-        last = larger(slice(384, 512), 1)
+        last = larger(slice(384, 512), 1, PACK)
         hand_on(o_b0, slice(0, 256), "o_w0", nc.sync)
         o_b2 = keep.tile([P, 128, PACK], BF16, tag="o_b0", align_bytes=64)
         dst, src = interleaved(o_b2[:], last[:])

from contextlib import ExitStack

import concourse.mybir as mybir

K, T, S, V, H = 512, 2048, 512, 512, 512
FLOPS = 3 * 2 * 512 * 512 * 512

F32 = mybir.dt.float32
BF16 = mybir.dt.bfloat16
I32 = mybir.dt.int32
U32 = mybir.dt.uint32
U16 = mybir.dt.uint16
U8 = mybir.dt.uint8
FP8X4 = mybir.dt.float8_e4m3fn_x4
ALU = mybir.AluOpType
ACT = mybir.ActivationFunctionType

P = 128
PACK = 4
HALF = 256
HALVES = [slice(0, HALF), slice(HALF, 2 * HALF)]


def entries(offsets, cols):
    return offsets[:, cols.start // 16 : cols.stop // 16]


def window(tile, offsets):
    return tile[:].rearrange("p h c -> p (h c)").indirect(offsets[:])


def as_words(dram):
    return dram[0].rearrange("p c r -> p (c r)").bitcast(I32)


def load_scale_rows(queue, plane, dram):
    for r in range(4):
        queue.dma_start(out=plane[r:P:32, :].bitcast(I32), in_=dram[0, r:16:4, :].bitcast(I32))


def deal(engine, out, in_, run):
    engine.tensor_copy(
        out=out.rearrange("p (t c i) -> p c t i", t=PACK, i=run),
        in_=in_.rearrange("p (c i t) -> p c t i", t=PACK, i=run),
    )


def interleaved(dst, src):
    return (
        dst.rearrange("p (c i) t -> p c t i", i=2),
        src.rearrange("p t (c i) -> p c t i", i=2),
    )


def tile_picked_keysq_none_po_kernel(
    tc, x_words, x_scales, w1_words, w1_scales, w2_words, w2_scales, ga, gb, offs, two, n1, nq, cq, out_0, out_1, out_2
):
    nc = tc.nc
    with ExitStack() as ctx:
        keep = ctx.enter_context(tc.tile_pool(name="keep", bufs=1))
        psum = ctx.enter_context(tc.psum_pool(name="psum", bufs=1))

        def list_tile(name, dram):
            tile = keep.tile([P, 32], U16, name=name)
            nc.sync.dma_start(tile[:], dram)
            return tile

        xs = keep.tile([P, T], U8, align_bytes=64)
        w1_s = keep.tile([P, H], U8, align_bytes=64)
        w2_s = keep.tile([P, H], U8, align_bytes=64, tag="early")
        nc.vector.memset(xs[:].bitcast(I32), 0)
        nc.vector.memset(w1_s[:].bitcast(I32), 0)
        nc.vector.memset(w2_s[:].bitcast(I32), 0)

        offs_t = list_tile("offs_t", offs)
        two_t = list_tile("two_t", two)
        ga_t = keep.tile([P, PACK], F32)
        gb_t = keep.tile([P, PACK], F32)
        nc.sync.dma_start(out=ga_t[:], in_=ga.rearrange("(p t) o -> p (t o)", t=PACK))
        nc.gpsimd.dma_start(out=gb_t[:], in_=gb.rearrange("(p t) o -> p (t o)", t=PACK))
        load_scale_rows(nc.sync, xs, x_scales)
        xw = keep.tile([P, T], I32, align_bytes=64)
        nc.sync.dma_start(out=xw[:], in_=as_words(x_words))
        load_scale_rows(nc.sync, w1_s, w1_scales)
        w1 = keep.tile([P, H], I32, align_bytes=64, tag="words")
        nc.sync.dma_start(out=w1[:], in_=as_words(w1_words))
        n1_t = list_tile("n1_t", n1)
        w2 = keep.tile([P, H], I32, align_bytes=64)
        nc.sync.dma_start(out=w2[:], in_=as_words(w2_words))
        load_scale_rows(nc.sync, w2_s, w2_scales)
        nq_t = list_tile("nq_t", nq)
        cq_t = list_tile("cq_t", cq)

        one_half = keep.tile([P, PACK], F32)
        nc.gpsimd.memset(one_half[:], 0.5)
        sign = keep.tile([P, PACK], F32)
        ga_abs = keep.tile([P, PACK], F32)
        ga_root = keep.tile([P, PACK], F32)
        nc.scalar.activation(ga_abs[:], ga_t[:], ACT.Abs)
        nc.scalar.activation(sign[:], ga_t[:], ACT.Sign)
        nc.gpsimd.tensor_tensor(ga_root[:], ga_abs[:], one_half[:], ALU.pow)
        a_win = [keep.tile([P, 2, S], F32, name="a_win%d" % t) for t in range(PACK)]
        b_win = [keep.tile([P, 2, V], F32, name="b_win%d" % t) for t in range(PACK)]
        for t in range(PACK):
            nc.scalar.activation(
                a_win[t][:, 1, :], gb_t[:, t : t + 1].to_broadcast([P, V]), ACT.Copy, scale=sign[:, t : t + 1]
            )

        xa_s = keep.tile([P, S], U8, align_bytes=64)
        xb_s = keep.tile([P, V], U8, align_bytes=64)
        xa_w = keep.tile([P, S], U32, align_bytes=64)
        w1_d = keep.tile([P, H], U32, align_bytes=64)
        w2_d = keep.tile([P, H], U32, align_bytes=64)
        w1_sd = keep.tile([P, H], U8, align_bytes=64)
        w2_sd = keep.tile([P, H], U8, align_bytes=64)
        nc.vector.tensor_copy(xa_s[:], xs[:].indirect(offs_t[:]))
        nc.vector.tensor_copy(xb_s[:], xs[:].indirect(two_t[:]))
        nc.vector.tensor_copy(xa_w[:], xw[:].bitcast(U32).indirect(offs_t[:]))
        deal(nc.vector, w1_sd[:], w1_s[:], 16)
        deal(nc.vector, w1_d[:], w1[:].bitcast(U32), 4)

        def project(bank, w_d, w_sd, x_w, x_s, t):
            cols = slice(P * t, P * (t + 1))
            nc.tensor.matmul_mx(
                out=bank[:],
                lhsT=w_d[:, cols].bitcast(FP8X4),
                lhsT_scale=w_sd[:, cols],
                rhs=x_w[:].bitcast(FP8X4),
                rhs_scale=x_s[:],
                start=True,
                stop=True,
            )

        for t in range(PACK):
            bank = psum.tile([P, S], F32, name="low%d" % t)
            project(bank, w1_d, w1_sd, xa_w, xa_s, t)
            nc.scalar.activation(a_win[t][:, 0, :], bank[:], ACT.Copy, scale=ga_root[:, t : t + 1])
            nc.scalar.activation(b_win[t][:, 1, :], bank[:], ACT.Copy, scale=ga_root[:, t : t + 1])

        xb_w = keep.tile([P, V], U32, align_bytes=64, tag="words")
        nc.vector.tensor_copy(xb_w[:], xw[:].bitcast(U32).indirect(two_t[:]))
        deal(nc.vector, w2_d[:], w2[:].bitcast(U32), 4)
        deal(nc.vector, w2_sd[:], w2_s[:], 16)
        for t in range(PACK):
            bank = psum.tile([P, V], F32, name="high%d" % t)
            project(bank, w2_d, w2_sd, xb_w, xb_s, t)
            nc.scalar.activation(b_win[t][:, 0, :], bank[:], ACT.Tanh)

        diff = keep.tile([P, PACK, S], F32, align_bytes=64, tag="early")
        for t in range(PACK):
            nc.vector.tensor_tensor(diff[:, t, :], window(a_win[t], n1_t), b_win[t][:, 1, :], ALU.subtract)
        z = [keep.tile([P, 2, P, PACK], BF16, name="z%d" % g, align_bytes=64) for g in range(2)]
        for g in range(2):
            nc.scalar.activation(
                z[g][:].rearrange("p u m t -> p m u t"),
                diff[:].rearrange("p t (m u) -> p m u t", u=PACK)[:, :, 2 * g : 2 * g + 2, :],
                ACT.Square,
            )

        z2_f = keep.tile([P, PACK, V], F32)
        for t in range(PACK):
            nc.vector.tensor_tensor(z2_f[:, t, :], window(b_win[t], nq_t), a_win[t][:, 1, :], ALU.mult)
        z2 = [keep.tile([P, HALF, PACK], BF16, name="z2_%d" % h, align_bytes=64) for h in range(2)]
        dst, src = interleaved(z2[1][:], z2_f[:, :, HALVES[1]])
        nc.scalar.activation(dst, src, ACT.Copy)
        dst, src = interleaved(z2[0][:], z2_f[:, :, HALVES[0]])
        nc.vector.tensor_copy(dst, src)

        def quantise(name, values, tag):
            words = keep.tile([P, HALF], U32, name=name + "_w", tag=tag, align_bytes=64)
            scales = keep.tile([P, HALF], U8, name=name + "_s", align_bytes=64)
            nc.vector.quantize_mx(out=words[:].bitcast(FP8X4), scales=scales[:], in_=values)
            return words, scales

        z_q = [quantise("zq0", z[0][:].rearrange("p u m t -> p (u m t)"), "zq0")]
        z2_q = [quantise("z2q0", z2[0][:].rearrange("p c t -> p (c t)"), "z0")]
        z2_q.append(quantise("z2q1", z2[1][:].rearrange("p c t -> p (c t)"), "z2q1"))
        z_q.append(quantise("zq1", z[1][:].rearrange("p u m t -> p (u m t)"), "z2_1"))

        s_win = [keep.tile([P, V], F32, name="s_win%d" % t) for t in range(PACK)]
        for t in range(PACK):
            rows = slice(P * (t % 2), P * (t % 2 + 1))
            for h, cols in enumerate(HALVES):
                bank = psum.tile([P, V], F32, name=("low%d", "high%d")[h] % t)
                nc.tensor.matmul_mx(
                    out=bank[:, 0:HALF],
                    lhsT=z_q[t // 2][0][:, rows].bitcast(FP8X4),
                    lhsT_scale=z_q[t // 2][1][:, rows],
                    rhs=z2_q[h][0][:].bitcast(FP8X4),
                    rhs_scale=z2_q[h][1][:],
                    start=True,
                    stop=True,
                )
                nc.scalar.activation(s_win[t][:, cols], bank[:, 0:HALF], ACT.Copy, scale=0.0625)

        out_rows = out_0.rearrange("(p t) v -> p t v", t=PACK)
        out_words = as_words(out_1)
        o_s = keep.tile([P, V], U8, align_bytes=64)

        def larger(cols, ring, tiles_a_store):
            width = cols.stop - cols.start
            o_f = keep.tile([P, PACK, width], F32, name="o_f%d" % cols.start)
            other = []
            for t in range(PACK + 1):
                if t < PACK:
                    other.append(keep.tile([P, width], F32, name="other%d" % ((ring + t) % 3)))
                    nc.vector.tensor_copy(other[t][:], s_win[t][:].indirect(entries(cq_t, cols)))
                if t > 0:
                    nc.vector.tensor_tensor(o_f[:, t - 1, :], other[t - 1][:], s_win[t - 1][:, cols], ALU.max)
                if t > 0 and t % tiles_a_store == 0:
                    done = slice(t - tiles_a_store, t)
                    nc.sync.dma_start(out=out_rows[:, done, cols], in_=o_f[:, done, :])
            return o_f

        def hand_on(o_b, cols, tag, queue):
            o_w = keep.tile([P, cols.stop - cols.start], U32, name="o_w", tag=tag, align_bytes=64)
            nc.vector.quantize_mx(
                out=o_w[:].bitcast(FP8X4), scales=o_s[:, cols], in_=o_b[:].rearrange("p c t -> p (c t)")
            )
            queue.dma_start(out=out_words[:, cols], in_=o_w[:].bitcast(I32))

        first = larger(slice(0, 384), 0, 1)
        o_b0 = keep.tile([P, 256, PACK], BF16, align_bytes=64)
        o_b1 = keep.tile([P, 128, PACK], BF16, align_bytes=64)
        dst, src = interleaved(o_b0[:], first[:, :, 0:256])
        nc.scalar.activation(dst, src, ACT.Copy)
        dst, src = interleaved(o_b1[:], first[:, :, 256:384])
        nc.scalar.activation(dst, src, ACT.Copy)
        last = larger(slice(384, 512), 1, PACK)
        hand_on(o_b0, slice(0, 256), "o_w0", nc.sync)
        o_b2 = keep.tile([P, 128, PACK], BF16, tag="o_b0", align_bytes=64)
        dst, src = interleaved(o_b2[:], last[:])
        nc.vector.tensor_copy(dst, src)
        hand_on(o_b1, slice(256, 384), "o_w1", nc.sync)
        hand_on(o_b2, slice(384, 512), "o_b1", nc.scalar)
        for r in range(4):
            (nc.sync, nc.scalar)[r % 2].dma_start(
                out=out_2[0, r:16:4, :].bitcast(I32), in_=o_s[r:P:32, :].bitcast(I32)
            )
